import numpy as np
import ml_dtypes


def mxq(x, axis, fmt="e4m3"):
    dtype, down = {"e4m3": (ml_dtypes.float8_e4m3fn, 7), "e5m2": (ml_dtypes.float8_e5m2, 14)}[fmt]
    v = np.moveaxis(np.asarray(x, np.float32).astype(ml_dtypes.bfloat16).astype(np.float64), axis, -1)
    blocks = v.reshape(v.shape[:-1] + (-1, 32))
    amax = np.abs(blocks).max(-1, keepdims=True)
    byte = np.maximum(np.where(amax > 0, np.frexp(amax)[1] - 1 + 127, 0) - down, 1)
    scale = np.exp2(byte - 127.0)
    codes = (blocks / scale).astype(np.float32).astype(dtype).astype(np.float64)
    return np.moveaxis((codes * scale).reshape(v.shape), -1, axis)


WIDE = False


def mx_kscale(k):
    if not WIDE:
        return np.ones(k)
    levels = np.array([10, -10, 5, -5, 0])
    if k % 512:
        return np.exp2(np.random.permutation(np.resize(levels, k // 32))).repeat(32)
    a = np.empty((k // 512, 16))
    for p in range(k // 512):
        a[p, :8] = np.random.permutation(np.resize(levels, 8))
        for g in range(8):
            far = levels[np.abs(levels - a[p, g]) >= 10]
            a[p, g + 8] = far[np.random.randint(len(far))]
    return np.exp2(a.ravel()).repeat(32)


def f64(x):
    return np.asarray(x).astype(np.float64)


def striped(idx):
    return np.tile(np.asarray(idx).reshape(-1, 16).T, (8, 1)).astype(np.uint16)


def unstriped(offs):
    return offs[:16].T.reshape(-1).astype(np.int64)


def striped8(idx):
    return np.asarray(idx).reshape(8, -1, 16).transpose(0, 2, 1).reshape(128, -1).astype(np.uint16)


def unstriped8(offs):
    return offs.reshape(8, 16, -1).transpose(0, 2, 1).reshape(8, -1).astype(np.int64)


def pick8(x, idx, run):
    r = np.arange(len(x))
    return x[r[:, None], idx[r % (8 * run) // run]]


E2M1 = np.array([0.0, 0.5, 1.0, 1.5, 2.0, 3.0, 4.0, 6.0, -0.0, -0.5, -1.0, -1.5, -2.0, -3.0, -4.0, -6.0])


def pack_weight(w, fmt):
    k, n = w.shape
    w = f64(np.asarray(w, np.float32).astype(ml_dtypes.bfloat16)).reshape(k // 32, 32, n)
    amax = np.abs(w).max(1)
    if fmt == "e4m3":
        byte = np.frexp(amax)[1] - 1 + 127 - 7
    else:
        mant, ex = np.frexp(amax / 6.0)
        byte = np.where(mant > 0.5, ex, ex - 1) + 127
    byte = np.clip(np.where(amax > 0, byte, 1), 1, 254)
    scaled = (w * np.exp2(127.0 - byte)[:, None, :]).reshape(k, n).astype(np.float32)
    by_word = np.ascontiguousarray(scaled.reshape(k // 512, 128, 4, n).transpose(0, 1, 3, 2))
    if fmt == "e4m3":
        words = by_word.astype(ml_dtypes.float8_e4m3fn).view(np.uint8)
    else:
        c = by_word.astype(ml_dtypes.float4_e2m1fn).view(np.uint8) & 0xF
        words = (c[..., 0::2] | (c[..., 1::2] << 4)).reshape(k // 512, 128, 2 * n)
    return np.ascontiguousarray(words), np.ascontiguousarray(byte.astype(np.uint8).reshape(k // 512, 16, n))


def unpack_weight(words, scales, fmt):
    g, _, n = scales.shape
    words = np.ascontiguousarray(words).reshape(g, 128, n, -1)
    if fmt == "e4m3":
        vals = words.view(ml_dtypes.float8_e4m3fn).astype(np.float64)
    else:
        nib = np.empty((g, 128, n, 4), np.uint8)
        nib[..., 0::2] = words & 0xF
        nib[..., 1::2] = words >> 4
        vals = E2M1[nib]
    vals = vals * np.repeat(np.exp2(scales.astype(np.float64) - 127.0), 8, axis=1)[..., None]
    return vals.transpose(0, 1, 3, 2).reshape(g * 512, n)


K, J, R, T, F, G, O, N, S, Z = 512, 256, 512, 1024, 1024, 1024, 128, 256, 512, 1024


def setup_inputs():
    n = np.random.standard_normal
    idx = np.stack([np.random.permutation(T)[:J] for _ in range(8)])
    idx2 = np.stack([np.random.permutation(T)[:J] for _ in range(8)])
    idx3 = np.random.permutation(F)[:R]
    idx4 = np.stack([np.random.permutation(G)[:R] for _ in range(8)])
    idx5 = np.stack([np.random.permutation(J)[:O] for _ in range(8)])
    idx6 = np.stack([np.random.permutation(J)[:O] for _ in range(8)])
    idx7 = np.random.permutation(Z)[:O]
    fk = mx_kscale(K)
    fr = mx_kscale(R)
    fs = mx_kscale(S)
    wbp = pack_weight(n((R, N)) * 1 / np.sqrt(R) / fr[:, None], "e2m1")
    xrp = pack_weight(n((S, Z)) / fs[:, None], "e4m3")
    wsp = pack_weight(n((S, N)) * 1 / np.sqrt(S) * fs[:, None], "e4m3")
    return {
        "ta": (np.random.randint(-7, 8, (K, T)).astype(np.float64)).astype(np.float32),
        "ga": ((np.random.randint(8, 19, (K, 1)) / 64.0) * fk[:, None]).astype(np.float32),
        "gb": ((np.random.randint(8, 19, (K, 1)) / 64.0) * fk[:, None]).astype(np.float32),
        "ua": (np.random.randint(-7, 8, (K, F)).astype(np.float64)).astype(np.float32),
        "ub": (np.random.randint(-7, 8, (K, G)).astype(np.float64)).astype(np.float32),
        "ha": ((np.random.randint(10, 25, (K, 1)) / 1024.0) / fk[:, None]).astype(np.float32),
        "hb": ((np.random.randint(4, 13, (K, 1)) / 1024.0) / fk[:, None]).astype(np.float32),
        "sa": (np.random.uniform(0.5, 1.6, (R, 1)) * fr[:, None]).astype(np.float32),
        "sb": (np.random.uniform(0.5, 1.6, (R, 1)) * fr[:, None]).astype(np.float32),
        "wb_words": wbp[0],
        "wb_scales": wbp[1],
        "xr_words": xrp[0],
        "xr_scales": xrp[1],
        "ws_words": wsp[0],
        "ws_scales": wsp[1],
        "offs": striped8(idx),
        "offs2": striped8(idx2),
        "offs3": striped(idx3),
        "offs4": striped8(idx4),
        "offs5": striped8(idx5),
        "offs6": striped8(idx6),
        "offs7": striped(idx7),
    }


def reference(ta, ga, gb, ua, ub, ha, hb, sa, sb, wb_words, wb_scales, xr_words, xr_scales, ws_words, ws_scales, offs, offs2, offs3, offs4, offs5, offs6, offs7):
    idx = unstriped8(offs)
    idx2 = unstriped8(offs2)
    idx3 = unstriped(offs3)
    idx4 = unstriped8(offs4)
    idx5 = unstriped8(offs5)
    idx6 = unstriped8(offs6)
    idx7 = unstriped(offs7)
    wbu = unpack_weight(wb_words, wb_scales, "e2m1")
    xru = unpack_weight(xr_words, xr_scales, "e4m3")
    wsu = unpack_weight(ws_words, ws_scales, "e4m3")
    xc = pick8(f64(ta), idx, 64) * f64(ga) - pick8(f64(ta), idx2, 64) * f64(gb)
    wc = f64(ua)[:, idx3] * f64(ha) + pick8(f64(ub), idx4, 64) * f64(hb)
    wcq = mxq(wc, 0, "e4m3")
    xcq = mxq(xc, 0, "e4m3")
    a = wcq.T @ xcq
    hid = np.maximum(pick8(a, idx5, 64) * f64(sa), pick8(a, idx6, 64) * f64(sb))
    hidq = mxq(hid, 0, "e4m3")
    xridx7g = xru[:, idx7]
    y = wbu.T @ hidq + wsu.T @ xridx7g
    return y

@@ -1,0 +1,206 @@
+from contextlib import ExitStack
+
+import concourse.mybir as mybir
+
+K, J, R, T, O, N, Z = 512, 256, 512, 1024, 128, 256, 1024
+FLOPS = 2 * (K * R * J + R * N * O + K * N * O)
+
+F32 = mybir.dt.float32
+BF16 = mybir.dt.bfloat16
+I32 = mybir.dt.int32
+U32 = mybir.dt.uint32
+U16 = mybir.dt.uint16
+U8 = mybir.dt.uint8
+FP8X4 = mybir.dt.float8_e4m3fn_x4
+FP4X4 = mybir.dt.float4_e2m1fn_x4
+COPY = mybir.ActivationFunctionType.Copy
+ALU = mybir.AluOpType
+
+P = 128
+PACK = 4
+PER_COLUMN = 16
+LAST_SLICE = 128
+
+
+def tile_picked_codegap_basedetail_one_grouppair_reminder_plain_kernel(
+    tc, ta, ga, gb, ua, ub, ha, hb, sa, sb, wb_words, wb_scales, xr_words, xr_scales,
+    ws_words, ws_scales, offs, offs2, offs3, offs4, offs5, offs6, offs7, out,
+):
+    nc = tc.nc
+    with ExitStack() as ctx:
+        keep = ctx.enter_context(tc.tile_pool(name="keep", bufs=1))
+        psum = ctx.enter_context(tc.psum_pool(name="psum", bufs=1))
+
+        def load_list(src, name):
+            tile = keep.tile(list(src.shape), U16, name=name)
+            nc.sync.dma_start(tile[:], src)
+            return tile
+
+        def load_steps(queue, src, name):
+            tile = keep.tile([P, PACK], F32, name=name)
+            queue.dma_start(tile[:], src.rearrange("(p j) o -> p (j o)", j=PACK))
+            return tile
+
+        def load_plane(src, j, name):
+            tile = keep.tile([P, T], F32, name=name)
+            nc.sync.dma_start(tile[:], src.rearrange("(p j) c -> p j c", j=PACK)[:, j, :])
+            return tile
+
+        def zeroed_scales(width, name):
+            tile = keep.tile([P, width], U8, name=name, align_bytes=64)
+            nc.vector.memset(tile[:].bitcast(I32), 0)
+            return tile
+
+        def load_scales(queue, tile, src):
+            for q in range(4):
+                queue.dma_start(
+                    tile[32 * q : 32 * q + 4, :].bitcast(I32),
+                    src[0, 4 * q : 4 * q + 4, :].bitcast(I32),
+                )
+
+        def fetch(dst, window, offsets, steps, j):
+            nc.scalar.activation(
+                out=dst, in_=window[:].indirect(offsets), func=COPY, scale=steps[:, j : j + 1]
+            )
+
+        ta_t, ua_t, ub_t = [], [], []
+        ta_t.append(load_plane(ta, 0, "ta0"))
+        l1 = load_list(offs, "l1")
+        ga_t = load_steps(nc.scalar, ga, "ga_t")
+        l2 = load_list(offs2, "l2")
+        gb_t = load_steps(nc.scalar, gb, "gb_t")
+        for j in range(1, PACK):
+            ta_t.append(load_plane(ta, j, "ta%d" % j))
+        l4 = load_list(offs4, "l4")
+        l3 = load_list(offs3, "l3")
+        hb_t = load_steps(nc.gpsimd, hb, "hb_t")
+        ha_t = load_steps(nc.gpsimd, ha, "ha_t")
+        for j in range(PACK):
+            ub_t.append(load_plane(ub, j, "ub%d" % j))
+            ua_t.append(load_plane(ua, j, "ua%d" % j))
+        sa_t = load_steps(nc.gpsimd, sa, "sa_t")
+        sb_t = load_steps(nc.gpsimd, sb, "sb_t")
+        xr_s = zeroed_scales(Z, "xr_s")
+        ws_s = zeroed_scales(N, "ws_s")
+        wb_s = zeroed_scales(N, "wb_s")
+        load_scales(nc.gpsimd, ws_s, ws_scales)
+        load_scales(nc.gpsimd, wb_s, wb_scales)
+        l5 = load_list(offs5, "l5")
+        l6 = load_list(offs6, "l6")
+        l7 = load_list(offs7, "l7")
+        xr_w = keep.tile([P, Z], I32, name="xr_w")
+        nc.sync.dma_start(xr_w[:], xr_words[0].rearrange("p n t -> p (n t)").bitcast(I32))
+        load_scales(nc.sync, xr_s, xr_scales)
+        ws_w = keep.tile([P, N], I32, name="ws_w", align_bytes=64)
+        nc.sync.dma_start(ws_w[:], ws_words[0].rearrange("p n t -> p (n t)").bitcast(I32))
+        wb_w = keep.tile([P, 2 * N], U8, name="wb_w", align_bytes=64)
+        nc.sync.dma_start(wb_w[:].bitcast(I32), wb_words[0].bitcast(I32))
+
+        xc = keep.tile([P, J * PACK], BF16, name="xc", align_bytes=64)
+        xc_v = xc[:].rearrange("p (c j) -> p c j", j=PACK)
+        for h in range(2):
+            first = keep.tile([P, 2, J], F32, name="x_first%d" % h)
+            second = keep.tile([P, 2, J], F32, name="x_second%d" % h)
+            for e in range(2):
+                j = 2 * h + e
+                fetch(first[:, e, :], ta_t[j], l1[:], ga_t, j)
+                fetch(second[:, e, :], ta_t[j], l2[:], gb_t, j)
+            nc.vector.tensor_tensor(
+                xc_v[:, :, 2 * h : 2 * h + 2],
+                first[:].rearrange("p e c -> p c e"),
+                second[:].rearrange("p e c -> p c e"),
+                ALU.subtract,
+            )
+        xc_w = keep.tile([P, J], U32, name="xc_w", align_bytes=64)
+        xc_s = keep.tile([P, J], U8, name="xc_s", align_bytes=64)
+        nc.vector.quantize_mx(out=xc_w[:].bitcast(FP8X4), scales=xc_s[:], in_=xc[:])
+
+        wc = keep.tile([P, R * PACK], BF16, name="wc", align_bytes=64)
+        wc_v = wc[:].rearrange("p (t m j) -> p m t j", t=PACK, j=PACK)
+        base01 = keep.tile([P, 2, R], F32, name="base01")
+        detail01 = keep.tile([P, 2, R], F32, name="detail01")
+        for j in range(2):
+            fetch(detail01[:, j, :], ub_t[j], l4[:], hb_t, j)
+            fetch(base01[:, j, :], ua_t[j], l3[:], ha_t, j)
+        nc.vector.tensor_tensor(
+            wc_v[:, :, :, 0:2],
+            base01[:].rearrange("p j (m t) -> p m t j", t=PACK),
+            detail01[:].rearrange("p j (m t) -> p m t j", t=PACK),
+            ALU.add,
+        )
+        for j, width in ((2, R), (3, LAST_SLICE)):
+            detail = keep.tile([P, R], F32, name="detail%d" % j)
+            fetch(detail[:], ub_t[j], l4[:], hb_t, j)
+            for r0 in range(0, R, width):
+                base = keep.tile([P, width], F32, name="base%d_%d" % (j, r0))
+                fetch(base[:], ua_t[j], l3[:, r0 // PER_COLUMN : (r0 + width) // PER_COLUMN], ha_t, j)
+                nc.vector.tensor_tensor(
+                    wc_v[:, r0 // PACK : (r0 + width) // PACK, :, j],
+                    base[:].rearrange("p (m t) -> p m t", t=PACK),
+                    detail[:, r0 : r0 + width].rearrange("p (m t) -> p m t", t=PACK),
+                    ALU.add,
+                )
+
+        a_t = []
+        for t in range(PACK):
+            wc_w = keep.tile([P, P], U32, name="wc_w%d" % t, align_bytes=64)
+            wc_s = keep.tile([P, P], U8, name="wc_s%d" % t, align_bytes=64)
+            nc.vector.quantize_mx(
+                out=wc_w[:].bitcast(FP8X4), scales=wc_s[:], in_=wc[:, t * R : (t + 1) * R]
+            )
+            acc = psum.tile([P, J], F32, name="acc_a%d" % t)
+            nc.tensor.matmul_mx(
+                out=acc[:], lhsT=wc_w[:].bitcast(FP8X4), lhsT_scale=wc_s[:],
+                rhs=xc_w[:].bitcast(FP8X4), rhs_scale=xc_s[:], start=True, stop=True,
+            )
+            a_t.append((acc, keep.tile([P, J], F32, name="a%d" % t)))
+        for t, (acc, a) in enumerate(a_t):
+            if t == 0:
+                nc.scalar.copy(a[:], acc[:])
+            else:
+                nc.vector.tensor_copy(a[:], acc[:])
+
+        xg_w = keep.tile([P, O], U32, name="xg_w", align_bytes=64)
+        xg_s = keep.tile([P, O], U8, name="xg_s", align_bytes=64)
+        nc.vector.tensor_copy(xg_w[:], xr_w[:].bitcast(U32).indirect(l7[:]))
+        nc.vector.tensor_copy(xg_s[:], xr_s[:].indirect(l7[:]))
+        acc_o = [psum.tile([P, O], F32, name="acc_o%d" % h) for h in range(2)]
+        for h in range(2):
+            nc.tensor.matmul_mx(
+                out=acc_o[h][:], lhsT=ws_w[:, h * P : (h + 1) * P].bitcast(FP8X4),
+                lhsT_scale=ws_s[:, h * P : (h + 1) * P],
+                rhs=xg_w[:].bitcast(FP8X4), rhs_scale=xg_s[:], start=True, stop=False,
+            )
+
+        hid = keep.tile([P, O * PACK], BF16, name="hid", align_bytes=64)
+        hid_v = hid[:].rearrange("p (c t) -> p c t", t=PACK)
+        for h in range(2):
+            first = keep.tile([P, 2, O], F32, name="h_first%d" % h)
+            second = keep.tile([P, 2, O], F32, name="h_second%d" % h)
+            for e in range(2):
+                t = 2 * h + e
+                fetch(first[:, e, :], a_t[t][1], l5[:], sa_t, t)
+                fetch(second[:, e, :], a_t[t][1], l6[:], sb_t, t)
+            nc.vector.tensor_tensor(
+                hid_v[:, :, 2 * h : 2 * h + 2],
+                first[:].rearrange("p e c -> p c e"),
+                second[:].rearrange("p e c -> p c e"),
+                ALU.max,
+            )
+        hid_w = keep.tile([P, O], U32, name="hid_w", align_bytes=64)
+        hid_s = keep.tile([P, O], U8, name="hid_s", align_bytes=64)
+        nc.vector.quantize_mx(out=hid_w[:].bitcast(FP8X4), scales=hid_s[:], in_=hid[:])
+
+        for h in range(2):
+            nc.tensor.matmul_mx(
+                out=acc_o[h][:], lhsT=wb_w[:, 2 * h * P : 2 * (h + 1) * P].bitcast(FP4X4),
+                lhsT_scale=wb_s[:, h * P : (h + 1) * P],
+                rhs=hid_w[:].bitcast(FP8X4), rhs_scale=hid_s[:], start=False, stop=True,
+            )
+            result = keep.tile([P, O], F32, name="result%d" % h)
+            if h == 0:
+                nc.vector.tensor_copy(result[:], acc_o[h][:])
+                nc.sync.dma_start(out[h * P : (h + 1) * P, :], result[:])
+            else:
+                nc.scalar.copy(result[:], acc_o[h][:])
+                nc.scalar.dma_start(out[h * P : (h + 1) * P, :], result[:])

@@ -20,6 +20,7 @@ P = 128
 PACK = 4
 PER_COLUMN = 16
 LAST_SLICE = 128
+LINE = 4
 
 
 def tile_picked_codegap_basedetail_one_grouppair_reminder_plain_kernel(
@@ -47,7 +48,7 @@ def tile_picked_codegap_basedetail_one_grouppair_reminder_plain_kernel(
             return tile
 
         def zeroed_scales(width, name):
-            tile = keep.tile([P, width], U8, name=name, align_bytes=64)
+            tile = keep.tile([P, width], U8, name=name, tag=name, align_bytes=64)
             nc.vector.memset(tile[:].bitcast(I32), 0)
             return tile
 
@@ -73,95 +74,99 @@ def tile_picked_codegap_basedetail_one_grouppair_reminder_plain_kernel(
             ta_t.append(load_plane(ta, j, "ta%d" % j))
         l4 = load_list(offs4, "l4")
         l3 = load_list(offs3, "l3")
-        hb_t = load_steps(nc.gpsimd, hb, "hb_t")
-        ha_t = load_steps(nc.gpsimd, ha, "ha_t")
+        hb_t = load_steps(nc.sync, hb, "hb_t")
+        ha_t = load_steps(nc.sync, ha, "ha_t")
         for j in range(PACK):
             ub_t.append(load_plane(ub, j, "ub%d" % j))
             ua_t.append(load_plane(ua, j, "ua%d" % j))
-        sa_t = load_steps(nc.gpsimd, sa, "sa_t")
-        sb_t = load_steps(nc.gpsimd, sb, "sb_t")
+        sa_t = load_steps(nc.sync, sa, "sa_t")
+        sb_t = load_steps(nc.sync, sb, "sb_t")
         xr_s = zeroed_scales(Z, "xr_s")
         ws_s = zeroed_scales(N, "ws_s")
         wb_s = zeroed_scales(N, "wb_s")
-        load_scales(nc.gpsimd, ws_s, ws_scales)
-        load_scales(nc.gpsimd, wb_s, wb_scales)
         l5 = load_list(offs5, "l5")
         l6 = load_list(offs6, "l6")
         l7 = load_list(offs7, "l7")
-        xr_w = keep.tile([P, Z], I32, name="xr_w")
+        xr_w = keep.tile([P, Z], I32, name="xr_w", tag="xr_w", align_bytes=64)
         nc.sync.dma_start(xr_w[:], xr_words[0].rearrange("p n t -> p (n t)").bitcast(I32))
         load_scales(nc.sync, xr_s, xr_scales)
         ws_w = keep.tile([P, N], I32, name="ws_w", align_bytes=64)
         nc.sync.dma_start(ws_w[:], ws_words[0].rearrange("p n t -> p (n t)").bitcast(I32))
+        load_scales(nc.sync, ws_s, ws_scales)
+        load_scales(nc.sync, wb_s, wb_scales)
         wb_w = keep.tile([P, 2 * N], U8, name="wb_w", align_bytes=64)
         nc.sync.dma_start(wb_w[:].bitcast(I32), wb_words[0].bitcast(I32))
 
+        x_first = keep.tile([P, PACK, J], F32, name="x_first")
+        x_second = keep.tile([P, PACK, J], F32, name="x_second")
+        for j in range(PACK):
+            fetch(x_first[:, j, :], ta_t[j], l1[:], ga_t, j)
+            fetch(x_second[:, j, :], ta_t[j], l2[:], gb_t, j)
         xc = keep.tile([P, J * PACK], BF16, name="xc", align_bytes=64)
-        xc_v = xc[:].rearrange("p (c j) -> p c j", j=PACK)
-        for h in range(2):
-            first = keep.tile([P, 2, J], F32, name="x_first%d" % h)
-            second = keep.tile([P, 2, J], F32, name="x_second%d" % h)
-            for e in range(2):
-                j = 2 * h + e
-                fetch(first[:, e, :], ta_t[j], l1[:], ga_t, j)
-                fetch(second[:, e, :], ta_t[j], l2[:], gb_t, j)
-            nc.vector.tensor_tensor(
-                xc_v[:, :, 2 * h : 2 * h + 2],
-                first[:].rearrange("p e c -> p c e"),
-                second[:].rearrange("p e c -> p c e"),
-                ALU.subtract,
-            )
+        nc.vector.tensor_tensor(
+            xc[:].rearrange("p (c i j) -> p c j i", i=LINE, j=PACK),
+            x_first[:].rearrange("p j (c i) -> p c j i", i=LINE),
+            x_second[:].rearrange("p j (c i) -> p c j i", i=LINE),
+            ALU.subtract,
+        )
         xc_w = keep.tile([P, J], U32, name="xc_w", align_bytes=64)
         xc_s = keep.tile([P, J], U8, name="xc_s", align_bytes=64)
         nc.vector.quantize_mx(out=xc_w[:].bitcast(FP8X4), scales=xc_s[:], in_=xc[:])
 
-        wc = keep.tile([P, R * PACK], BF16, name="wc", align_bytes=64)
-        wc_v = wc[:].rearrange("p (t m j) -> p m t j", t=PACK, j=PACK)
-        base01 = keep.tile([P, 2, R], F32, name="base01")
-        detail01 = keep.tile([P, 2, R], F32, name="detail01")
-        for j in range(2):
-            fetch(detail01[:, j, :], ub_t[j], l4[:], hb_t, j)
-            fetch(base01[:, j, :], ua_t[j], l3[:], ha_t, j)
-        nc.vector.tensor_tensor(
-            wc_v[:, :, :, 0:2],
-            base01[:].rearrange("p j (m t) -> p m t j", t=PACK),
-            detail01[:].rearrange("p j (m t) -> p m t j", t=PACK),
-            ALU.add,
-        )
-        for j, width in ((2, R), (3, LAST_SLICE)):
-            detail = keep.tile([P, R], F32, name="detail%d" % j)
-            fetch(detail[:], ub_t[j], l4[:], hb_t, j)
+        pairs = keep.tile([P, PACK * R], BF16, name="pairs")
+        pairs_v = pairs[:].rearrange("p (h t m e) -> p h m e t", h=2, t=PACK, e=2)
+        for h in range(2):
+            base = keep.tile([P, 2, R], F32, name="base%d" % h)
+            detail = keep.tile([P, 2, R], F32, name="detail%d" % h)
+            fetch(detail[:, 0, :], ub_t[2 * h], l4[:], hb_t, 2 * h)
+            fetch(base[:, 0, :], ua_t[2 * h], l3[:], ha_t, 2 * h)
+            fetch(detail[:, 1, :], ub_t[2 * h + 1], l4[:], hb_t, 2 * h + 1)
+            width = R if h == 0 else LAST_SLICE
             for r0 in range(0, R, width):
-                base = keep.tile([P, width], F32, name="base%d_%d" % (j, r0))
-                fetch(base[:], ua_t[j], l3[:, r0 // PER_COLUMN : (r0 + width) // PER_COLUMN], ha_t, j)
+                cols = slice(r0, r0 + width)
+                fetch(base[:, 1, cols], ua_t[2 * h + 1],
+                      l3[:, r0 // PER_COLUMN : (r0 + width) // PER_COLUMN], ha_t, 2 * h + 1)
                 nc.vector.tensor_tensor(
-                    wc_v[:, r0 // PACK : (r0 + width) // PACK, :, j],
-                    base[:].rearrange("p (m t) -> p m t", t=PACK),
-                    detail[:, r0 : r0 + width].rearrange("p (m t) -> p m t", t=PACK),
+                    pairs_v[:, h, r0 // PACK : (r0 + width) // PACK],
+                    base[:, :, cols].rearrange("p e (m t) -> p m e t", t=PACK),
+                    detail[:, :, cols].rearrange("p e (m t) -> p m e t", t=PACK),
                     ALU.add,
                 )
 
-        a_t = []
-        for t in range(PACK):
+        pair_words = pairs[:].bitcast(I32).rearrange("p (h t m i) -> p t m h i", h=2, t=PACK, i=LINE)
+        wc_t, a_t = [], []
+
+        def weave(t):
+            wc = keep.tile([P, P * PACK], BF16, name="wc%d" % t, align_bytes=64, tag="wc%d" % t)
+            nc.vector.tensor_copy(
+                wc[:].bitcast(I32).rearrange("p (m i h) -> p m h i", i=LINE, h=2), pair_words[:, t]
+            )
+            wc_t.append(wc)
+
+        def first_product(t):
             wc_w = keep.tile([P, P], U32, name="wc_w%d" % t, align_bytes=64)
             wc_s = keep.tile([P, P], U8, name="wc_s%d" % t, align_bytes=64)
-            nc.vector.quantize_mx(
-                out=wc_w[:].bitcast(FP8X4), scales=wc_s[:], in_=wc[:, t * R : (t + 1) * R]
-            )
+            nc.vector.quantize_mx(out=wc_w[:].bitcast(FP8X4), scales=wc_s[:], in_=wc_t[t][:])
             acc = psum.tile([P, J], F32, name="acc_a%d" % t)
             nc.tensor.matmul_mx(
                 out=acc[:], lhsT=wc_w[:].bitcast(FP8X4), lhsT_scale=wc_s[:],
                 rhs=xc_w[:].bitcast(FP8X4), rhs_scale=xc_s[:], start=True, stop=True,
             )
             a_t.append((acc, keep.tile([P, J], F32, name="a%d" % t)))
+
+        weave(0)
+        for t in range(PACK):
+            if t + 1 < PACK:
+                weave(t + 1)
+            first_product(t)
         for t, (acc, a) in enumerate(a_t):
             if t == 0:
                 nc.scalar.copy(a[:], acc[:])
             else:
                 nc.vector.tensor_copy(a[:], acc[:])
 
-        xg_w = keep.tile([P, O], U32, name="xg_w", align_bytes=64)
-        xg_s = keep.tile([P, O], U8, name="xg_s", align_bytes=64)
+        xg_w = keep.tile([P, O], U32, name="xg_w", align_bytes=64, tag="wc2")
+        xg_s = keep.tile([P, O], U8, name="xg_s", align_bytes=64, tag="wc3")
         nc.vector.tensor_copy(xg_w[:], xr_w[:].bitcast(U32).indirect(l7[:]))
         nc.vector.tensor_copy(xg_s[:], xr_s[:].indirect(l7[:]))
         acc_o = [psum.tile([P, O], F32, name="acc_o%d" % h) for h in range(2)]
@@ -172,24 +177,27 @@ def tile_picked_codegap_basedetail_one_grouppair_reminder_plain_kernel(
                 rhs=xg_w[:].bitcast(FP8X4), rhs_scale=xg_s[:], start=True, stop=False,
             )
 
-        hid = keep.tile([P, O * PACK], BF16, name="hid", align_bytes=64)
-        hid_v = hid[:].rearrange("p (c t) -> p c t", t=PACK)
-        for h in range(2):
-            first = keep.tile([P, 2, O], F32, name="h_first%d" % h)
-            second = keep.tile([P, 2, O], F32, name="h_second%d" % h)
-            for e in range(2):
-                t = 2 * h + e
-                fetch(first[:, e, :], a_t[t][1], l5[:], sa_t, t)
-                fetch(second[:, e, :], a_t[t][1], l6[:], sb_t, t)
-            nc.vector.tensor_tensor(
-                hid_v[:, :, 2 * h : 2 * h + 2],
-                first[:].rearrange("p e c -> p c e"),
-                second[:].rearrange("p e c -> p c e"),
-                ALU.max,
-            )
+        h_first = keep.tile([P, PACK, O], F32, name="h_first")
+        h_second = keep.tile([P, PACK, O], F32, name="h_second")
+        for t in range(PACK - 1):
+            fetch(h_first[:, t, :], a_t[t][1], l5[:], sa_t, t)
+            fetch(h_second[:, t, :], a_t[t][1], l6[:], sb_t, t)
         hid_w = keep.tile([P, O], U32, name="hid_w", align_bytes=64)
         hid_s = keep.tile([P, O], U8, name="hid_s", align_bytes=64)
-        nc.vector.quantize_mx(out=hid_w[:].bitcast(FP8X4), scales=hid_s[:], in_=hid[:])
+        half = O // 2
+        for h in range(2):
+            cols = slice(h * half, (h + 1) * half)
+            entries = slice(h * half // PER_COLUMN, (h + 1) * half // PER_COLUMN)
+            fetch(h_first[:, PACK - 1, cols], a_t[PACK - 1][1], l5[:, entries], sa_t, PACK - 1)
+            fetch(h_second[:, PACK - 1, cols], a_t[PACK - 1][1], l6[:, entries], sb_t, PACK - 1)
+            hid = keep.tile([P, half * PACK], BF16, name="hid%d" % h, align_bytes=64, tag=("xr_w", "xr_s")[h])
+            nc.vector.tensor_tensor(
+                hid[:].rearrange("p (c i t) -> p c t i", i=LINE, t=PACK),
+                h_first[:, :, cols].rearrange("p t (c i) -> p c t i", i=LINE),
+                h_second[:, :, cols].rearrange("p t (c i) -> p c t i", i=LINE),
+                ALU.max,
+            )
+            nc.vector.quantize_mx(out=hid_w[:, cols].bitcast(FP8X4), scales=hid_s[:, cols], in_=hid[:])
 
         for h in range(2):
             nc.tensor.matmul_mx(

@@ -64,6 +64,11 @@ def tile_picked_codegap_basedetail_one_grouppair_reminder_plain_kernel(
                 out=dst, in_=window[:].indirect(offsets), func=COPY, scale=steps[:, j : j + 1]
             )
 
+        warm_in = keep.tile([P, 2], F32, name="warm_in")
+        warm_out = keep.tile([P, 2], F32, name="warm_out")
+        nc.vector.memset(warm_in[:], 0.0)
+        nc.scalar.activation(out=warm_out[:], in_=warm_in[:], func=COPY)
+
         ta_t, ua_t, ub_t = [], [], []
         ta_t.append(load_plane(ta, 0, "ta0"))
         l1 = load_list(offs, "l1")

@@ -19,7 +19,8 @@ ALU = mybir.AluOpType
 P = 128
 PACK = 4
 PER_COLUMN = 16
-LAST_SLICE = 128
+CUT_A, CUT_B = 256, 448
+CUT_T1 = 128
 LINE = 4
 
 
@@ -47,17 +48,15 @@ def tile_picked_codegap_basedetail_one_grouppair_reminder_plain_kernel(
             nc.sync.dma_start(tile[:], src.rearrange("(p j) c -> p j c", j=PACK)[:, j, :])
             return tile
 
-        def zeroed_scales(width, name):
-            tile = keep.tile([P, width], U8, name=name, tag=name, align_bytes=64)
-            nc.vector.memset(tile[:].bitcast(I32), 0)
-            return tile
-
-        def load_scales(queue, tile, src):
+        def load_scale_rows(src, name):
+            width = src.shape[2]
+            staged = keep.tile([4, 4, width // 4], I32, name=name + "_staged")
+            nc.sync.dma_start(staged[:], src[0].bitcast(I32).rearrange("(q i) w -> i q w", i=4))
+            plane = keep.tile([P, width], U8, name=name, tag=name, align_bytes=64)
+            nc.vector.memset(plane[:].bitcast(I32), 0)
             for q in range(4):
-                queue.dma_start(
-                    tile[32 * q : 32 * q + 4, :].bitcast(I32),
-                    src[0, 4 * q : 4 * q + 4, :].bitcast(I32),
-                )
+                nc.vector.tensor_copy(plane[32 * q : 32 * q + 4, :].bitcast(I32), staged[:, q, :])
+            return plane
 
         def fetch(dst, window, offsets, steps, j):
             nc.scalar.activation(
@@ -75,30 +74,33 @@ def tile_picked_codegap_basedetail_one_grouppair_reminder_plain_kernel(
         ga_t = load_steps(nc.scalar, ga, "ga_t")
         l2 = load_list(offs2, "l2")
         gb_t = load_steps(nc.scalar, gb, "gb_t")
-        for j in range(1, PACK):
-            ta_t.append(load_plane(ta, j, "ta%d" % j))
+        ta_t.append(load_plane(ta, 1, "ta1"))
+        ta_t.append(load_plane(ta, 2, "ta2"))
         l4 = load_list(offs4, "l4")
-        l3 = load_list(offs3, "l3")
         hb_t = load_steps(nc.sync, hb, "hb_t")
+        ta_t.append(load_plane(ta, 3, "ta3"))
+        l3 = load_list(offs3, "l3")
         ha_t = load_steps(nc.sync, ha, "ha_t")
-        for j in range(PACK):
-            ub_t.append(load_plane(ub, j, "ub%d" % j))
-            ua_t.append(load_plane(ua, j, "ua%d" % j))
-        sa_t = load_steps(nc.sync, sa, "sa_t")
-        sb_t = load_steps(nc.sync, sb, "sb_t")
-        xr_s = zeroed_scales(Z, "xr_s")
-        ws_s = zeroed_scales(N, "ws_s")
-        wb_s = zeroed_scales(N, "wb_s")
-        l5 = load_list(offs5, "l5")
-        l6 = load_list(offs6, "l6")
+        ub_t.append(load_plane(ub, 0, "ub0"))
+        xr_s = load_scale_rows(xr_scales, "xr_s")
+        ua_t.append(load_plane(ua, 0, "ua0"))
+        ws_s = load_scale_rows(ws_scales, "ws_s")
+        ub_t.append(load_plane(ub, 1, "ub1"))
+        wb_s = load_scale_rows(wb_scales, "wb_s")
+        ua_t.append(load_plane(ua, 1, "ua1"))
         l7 = load_list(offs7, "l7")
+        sa_t = load_steps(nc.sync, sa, "sa_t")
+        ub_t.append(load_plane(ub, 2, "ub2"))
+        l5 = load_list(offs5, "l5")
+        sb_t = load_steps(nc.sync, sb, "sb_t")
+        ua_t.append(load_plane(ua, 2, "ua2"))
+        l6 = load_list(offs6, "l6")
+        ub_t.append(load_plane(ub, 3, "ub3"))
+        ua_t.append(load_plane(ua, 3, "ua3"))
         xr_w = keep.tile([P, Z], I32, name="xr_w", tag="xr_w", align_bytes=64)
         nc.sync.dma_start(xr_w[:], xr_words[0].rearrange("p n t -> p (n t)").bitcast(I32))
-        load_scales(nc.sync, xr_s, xr_scales)
         ws_w = keep.tile([P, N], I32, name="ws_w", align_bytes=64)
         nc.sync.dma_start(ws_w[:], ws_words[0].rearrange("p n t -> p (n t)").bitcast(I32))
-        load_scales(nc.sync, ws_s, ws_scales)
-        load_scales(nc.sync, wb_s, wb_scales)
         wb_w = keep.tile([P, 2 * N], U8, name="wb_w", align_bytes=64)
         nc.sync.dma_start(wb_w[:].bitcast(I32), wb_words[0].bitcast(I32))
 
@@ -118,40 +120,52 @@ def tile_picked_codegap_basedetail_one_grouppair_reminder_plain_kernel(
         xc_s = keep.tile([P, J], U8, name="xc_s", align_bytes=64)
         nc.vector.quantize_mx(out=xc_w[:].bitcast(FP8X4), scales=xc_s[:], in_=xc[:])
 
-        pairs = keep.tile([P, PACK * R], BF16, name="pairs")
-        pairs_v = pairs[:].rearrange("p (h t m e) -> p h m e t", h=2, t=PACK, e=2)
-        for h in range(2):
-            base = keep.tile([P, 2, R], F32, name="base%d" % h)
-            detail = keep.tile([P, 2, R], F32, name="detail%d" % h)
-            fetch(detail[:, 0, :], ub_t[2 * h], l4[:], hb_t, 2 * h)
-            fetch(base[:, 0, :], ua_t[2 * h], l3[:], ha_t, 2 * h)
-            fetch(detail[:, 1, :], ub_t[2 * h + 1], l4[:], hb_t, 2 * h + 1)
-            width = R if h == 0 else LAST_SLICE
-            for r0 in range(0, R, width):
-                cols = slice(r0, r0 + width)
-                fetch(base[:, 1, cols], ua_t[2 * h + 1],
-                      l3[:, r0 // PER_COLUMN : (r0 + width) // PER_COLUMN], ha_t, 2 * h + 1)
-                nc.vector.tensor_tensor(
-                    pairs_v[:, h, r0 // PACK : (r0 + width) // PACK],
-                    base[:, :, cols].rearrange("p e (m t) -> p m e t", t=PACK),
-                    detail[:, :, cols].rearrange("p e (m t) -> p m e t", t=PACK),
-                    ALU.add,
-                )
+        wc = keep.tile([P, PACK * R], BF16, name="wc", tag="wc", align_bytes=64)
+        wc_v = wc[:].rearrange("p (t m j) -> p m j t", t=PACK, j=PACK)
+        base01 = keep.tile([P, 2, R], F32, name="base01")
+        detail01 = keep.tile([P, 2, R], F32, name="detail01")
+        for j in range(2):
+            fetch(detail01[:, j, :], ub_t[j], l4[:], hb_t, j)
+            fetch(base01[:, j, :], ua_t[j], l3[:], ha_t, j)
+        nc.vector.tensor_tensor(
+            wc_v[:, :, 0:2, :],
+            base01[:].rearrange("p j (m t) -> p m j t", t=PACK),
+            detail01[:].rearrange("p j (m t) -> p m j t", t=PACK),
+            ALU.add,
+        )
+        base2 = keep.tile([P, R], F32, name="base2")
+        detail2 = keep.tile([P, R], F32, name="detail2")
+        fetch(detail2[:], ub_t[2], l4[:], hb_t, 2)
+        fetch(base2[:], ua_t[2], l3[:], ha_t, 2)
+        nc.vector.tensor_tensor(
+            wc_v[:, :, 2, :],
+            base2[:].rearrange("p (m t) -> p m t", t=PACK),
+            detail2[:].rearrange("p (m t) -> p m t", t=PACK),
+            ALU.add,
+        )
+        base3 = keep.tile([P, R], F32, name="base3")
+        detail3 = keep.tile([P, R], F32, name="detail3")
+        fetch(detail3[:], ub_t[3], l4[:], hb_t, 3)
 
-        pair_words = pairs[:].bitcast(I32).rearrange("p (h t m i) -> p t m h i", h=2, t=PACK, i=LINE)
-        wc_t, a_t = [], []
+        def fetch_base3(r0, r1):
+            fetch(base3[:, r0:r1], ua_t[3], l3[:, r0 // PER_COLUMN : r1 // PER_COLUMN], ha_t, 3)
 
-        def weave(t):
-            wc = keep.tile([P, P * PACK], BF16, name="wc%d" % t, align_bytes=64, tag="wc%d" % t)
-            nc.vector.tensor_copy(
-                wc[:].bitcast(I32).rearrange("p (m i h) -> p m h i", i=LINE, h=2), pair_words[:, t]
+        def add_last(t, r0, r1):
+            nc.vector.tensor_tensor(
+                wc_v[:, r0 // PACK : r1 // PACK, 3, t],
+                base3[:, r0 + t : r1 : PACK],
+                detail3[:, r0 + t : r1 : PACK],
+                ALU.add,
             )
-            wc_t.append(wc)
+
+        a_t = []
 
         def first_product(t):
             wc_w = keep.tile([P, P], U32, name="wc_w%d" % t, align_bytes=64)
             wc_s = keep.tile([P, P], U8, name="wc_s%d" % t, align_bytes=64)
-            nc.vector.quantize_mx(out=wc_w[:].bitcast(FP8X4), scales=wc_s[:], in_=wc_t[t][:])
+            nc.vector.quantize_mx(
+                out=wc_w[:].bitcast(FP8X4), scales=wc_s[:], in_=wc[:, t * R : (t + 1) * R]
+            )
             acc = psum.tile([P, J], F32, name="acc_a%d" % t)
             nc.tensor.matmul_mx(
                 out=acc[:], lhsT=wc_w[:].bitcast(FP8X4), lhsT_scale=wc_s[:],
@@ -159,19 +173,28 @@ def tile_picked_codegap_basedetail_one_grouppair_reminder_plain_kernel(
             )
             a_t.append((acc, keep.tile([P, J], F32, name="a%d" % t)))
 
-        weave(0)
-        for t in range(PACK):
-            if t + 1 < PACK:
-                weave(t + 1)
-            first_product(t)
+        fetch_base3(0, CUT_A)
+        add_last(0, 0, CUT_A)
+        add_last(1, 0, CUT_T1)
+        fetch_base3(CUT_A, CUT_B)
+        add_last(0, CUT_A, CUT_B)
+        fetch_base3(CUT_B, R)
+        add_last(0, CUT_B, R)
+        add_last(1, CUT_T1, R)
+        first_product(0)
+        first_product(1)
+        add_last(2, 0, R)
+        add_last(3, 0, R)
+        first_product(2)
+        first_product(3)
         for t, (acc, a) in enumerate(a_t):
             if t == 0:
                 nc.scalar.copy(a[:], acc[:])
             else:
                 nc.vector.tensor_copy(a[:], acc[:])
 
-        xg_w = keep.tile([P, O], U32, name="xg_w", align_bytes=64, tag="wc2")
-        xg_s = keep.tile([P, O], U8, name="xg_s", align_bytes=64, tag="wc3")
+        xg_w = keep.tile([P, O], U32, name="xg_w", align_bytes=64, tag="wc")
+        xg_s = keep.tile([P, O], U8, name="xg_s", align_bytes=64)
         nc.vector.tensor_copy(xg_w[:], xr_w[:].bitcast(U32).indirect(l7[:]))
         nc.vector.tensor_copy(xg_s[:], xr_s[:].indirect(l7[:]))
         acc_o = [psum.tile([P, O], F32, name="acc_o%d" % h) for h in range(2)]
@@ -189,20 +212,28 @@ def tile_picked_codegap_basedetail_one_grouppair_reminder_plain_kernel(
             fetch(h_second[:, t, :], a_t[t][1], l6[:], sb_t, t)
         hid_w = keep.tile([P, O], U32, name="hid_w", align_bytes=64)
         hid_s = keep.tile([P, O], U8, name="hid_s", align_bytes=64)
-        half = O // 2
-        for h in range(2):
-            cols = slice(h * half, (h + 1) * half)
-            entries = slice(h * half // PER_COLUMN, (h + 1) * half // PER_COLUMN)
-            fetch(h_first[:, PACK - 1, cols], a_t[PACK - 1][1], l5[:, entries], sa_t, PACK - 1)
-            fetch(h_second[:, PACK - 1, cols], a_t[PACK - 1][1], l6[:, entries], sb_t, PACK - 1)
-            hid = keep.tile([P, half * PACK], BF16, name="hid%d" % h, align_bytes=64, tag=("xr_w", "xr_s")[h])
+        half, last = O // 2, PACK - 1
+        halves = [slice(h * half, (h + 1) * half) for h in range(2)]
+        hid = [
+            keep.tile([P, half * PACK], BF16, name="hid%d" % h, align_bytes=64, tag=("xr_w", "xr_s")[h])
+            for h in range(2)
+        ]
+        for h, cols in enumerate(halves):
             nc.vector.tensor_tensor(
-                hid[:].rearrange("p (c i t) -> p c t i", i=LINE, t=PACK),
-                h_first[:, :, cols].rearrange("p t (c i) -> p c t i", i=LINE),
-                h_second[:, :, cols].rearrange("p t (c i) -> p c t i", i=LINE),
+                hid[h][:].rearrange("p (c i t) -> p c t i", i=LINE, t=PACK)[:, :, 0:last, :],
+                h_first[:, 0:last, cols].rearrange("p t (c i) -> p c t i", i=LINE),
+                h_second[:, 0:last, cols].rearrange("p t (c i) -> p c t i", i=LINE),
                 ALU.max,
             )
-            nc.vector.quantize_mx(out=hid_w[:, cols].bitcast(FP8X4), scales=hid_s[:, cols], in_=hid[:])
+        fetch(h_first[:, last, :], a_t[last][1], l5[:], sa_t, last)
+        for h, cols in enumerate(halves):
+            entries = slice(h * half // PER_COLUMN, (h + 1) * half // PER_COLUMN)
+            fetch(h_second[:, last, cols], a_t[last][1], l6[:, entries], sb_t, last)
+            nc.vector.tensor_tensor(
+                hid[h][:, last::PACK], h_first[:, last, cols], h_second[:, last, cols], ALU.max
+            )
+        for h, cols in enumerate(halves):
+            nc.vector.quantize_mx(out=hid_w[:, cols].bitcast(FP8X4), scales=hid_s[:, cols], in_=hid[h][:])
 
         for h in range(2):
             nc.tensor.matmul_mx(

from contextlib import ExitStack

import concourse.mybir as mybir

K, J, R, T, O, N, Z = 512, 256, 512, 1024, 128, 256, 1024
FLOPS = 2 * (K * R * J + R * N * O + K * N * O)

F32 = mybir.dt.float32
BF16 = mybir.dt.bfloat16
I32 = mybir.dt.int32
U32 = mybir.dt.uint32
U16 = mybir.dt.uint16
U8 = mybir.dt.uint8
FP8X4 = mybir.dt.float8_e4m3fn_x4
FP4X4 = mybir.dt.float4_e2m1fn_x4
COPY = mybir.ActivationFunctionType.Copy
ALU = mybir.AluOpType

P = 128
PACK = 4
PER_COLUMN = 16
CUT_A, CUT_B = 256, 448
CUT_T1 = 128
LINE = 4


def tile_picked_codegap_basedetail_one_grouppair_reminder_plain_kernel(
    tc, ta, ga, gb, ua, ub, ha, hb, sa, sb, wb_words, wb_scales, xr_words, xr_scales,
    ws_words, ws_scales, offs, offs2, offs3, offs4, offs5, offs6, offs7, out,
):
    nc = tc.nc
    with ExitStack() as ctx:
        keep = ctx.enter_context(tc.tile_pool(name="keep", bufs=1))
        psum = ctx.enter_context(tc.psum_pool(name="psum", bufs=1))

        def load_list(src, name):
            tile = keep.tile(list(src.shape), U16, name=name)
            nc.sync.dma_start(tile[:], src)
            return tile

        def load_steps(queue, src, name):
            tile = keep.tile([P, PACK], F32, name=name)
            queue.dma_start(tile[:], src.rearrange("(p j) o -> p (j o)", j=PACK))
            return tile

        def load_plane(src, j, name):
            tile = keep.tile([P, T], F32, name=name)
            nc.sync.dma_start(tile[:], src.rearrange("(p j) c -> p j c", j=PACK)[:, j, :])
            return tile

        def load_scale_rows(src, name):
            width = src.shape[2]
            staged = keep.tile([4, 4, width // 4], I32, name=name + "_staged")
            nc.sync.dma_start(staged[:], src[0].bitcast(I32).rearrange("(q i) w -> i q w", i=4))
            plane = keep.tile([P, width], U8, name=name, tag=name, align_bytes=64)
            nc.vector.memset(plane[:].bitcast(I32), 0)
            for q in range(4):
                nc.vector.tensor_copy(plane[32 * q : 32 * q + 4, :].bitcast(I32), staged[:, q, :])
            return plane

        def fetch(dst, window, offsets, steps, j):
            nc.scalar.activation(
                out=dst, in_=window[:].indirect(offsets), func=COPY, scale=steps[:, j : j + 1]
            )

        warm_in = keep.tile([P, 2], F32, name="warm_in")
        warm_out = keep.tile([P, 2], F32, name="warm_out")
        nc.vector.memset(warm_in[:], 0.0)
        nc.scalar.activation(out=warm_out[:], in_=warm_in[:], func=COPY)

        ta_t, ua_t, ub_t = [], [], []
        ta_t.append(load_plane(ta, 0, "ta0"))
        l1 = load_list(offs, "l1")
        ga_t = load_steps(nc.scalar, ga, "ga_t")
        l2 = load_list(offs2, "l2")
        gb_t = load_steps(nc.scalar, gb, "gb_t")
        ta_t.append(load_plane(ta, 1, "ta1"))
        ta_t.append(load_plane(ta, 2, "ta2"))
        l4 = load_list(offs4, "l4")
        hb_t = load_steps(nc.sync, hb, "hb_t")
        ta_t.append(load_plane(ta, 3, "ta3"))
        l3 = load_list(offs3, "l3")
        ha_t = load_steps(nc.sync, ha, "ha_t")
        ub_t.append(load_plane(ub, 0, "ub0"))
        xr_s = load_scale_rows(xr_scales, "xr_s")
        ua_t.append(load_plane(ua, 0, "ua0"))
        ws_s = load_scale_rows(ws_scales, "ws_s")
        ub_t.append(load_plane(ub, 1, "ub1"))
        wb_s = load_scale_rows(wb_scales, "wb_s")
        ua_t.append(load_plane(ua, 1, "ua1"))
        l7 = load_list(offs7, "l7")
        sa_t = load_steps(nc.sync, sa, "sa_t")
        ub_t.append(load_plane(ub, 2, "ub2"))
        l5 = load_list(offs5, "l5")
        sb_t = load_steps(nc.sync, sb, "sb_t")
        ua_t.append(load_plane(ua, 2, "ua2"))
        l6 = load_list(offs6, "l6")
        ub_t.append(load_plane(ub, 3, "ub3"))
        ua_t.append(load_plane(ua, 3, "ua3"))
        xr_w = keep.tile([P, Z], I32, name="xr_w", tag="xr_w", align_bytes=64)
        nc.sync.dma_start(xr_w[:], xr_words[0].rearrange("p n t -> p (n t)").bitcast(I32))
        ws_w = keep.tile([P, N], I32, name="ws_w", align_bytes=64)
        nc.sync.dma_start(ws_w[:], ws_words[0].rearrange("p n t -> p (n t)").bitcast(I32))
        wb_w = keep.tile([P, 2 * N], U8, name="wb_w", align_bytes=64)
        nc.sync.dma_start(wb_w[:].bitcast(I32), wb_words[0].bitcast(I32))

        x_first = keep.tile([P, PACK, J], F32, name="x_first")
        x_second = keep.tile([P, PACK, J], F32, name="x_second")
        for j in range(PACK):
            fetch(x_first[:, j, :], ta_t[j], l1[:], ga_t, j)
            fetch(x_second[:, j, :], ta_t[j], l2[:], gb_t, j)
        xc = keep.tile([P, J * PACK], BF16, name="xc", align_bytes=64)
        nc.vector.tensor_tensor(
            xc[:].rearrange("p (c i j) -> p c j i", i=LINE, j=PACK),
            x_first[:].rearrange("p j (c i) -> p c j i", i=LINE),
            x_second[:].rearrange("p j (c i) -> p c j i", i=LINE),
            ALU.subtract,
        )
        xc_w = keep.tile([P, J], U32, name="xc_w", align_bytes=64)
        xc_s = keep.tile([P, J], U8, name="xc_s", align_bytes=64)
        nc.vector.quantize_mx(out=xc_w[:].bitcast(FP8X4), scales=xc_s[:], in_=xc[:])

        wc = keep.tile([P, PACK * R], BF16, name="wc", tag="wc", align_bytes=64)
        wc_v = wc[:].rearrange("p (t m j) -> p m j t", t=PACK, j=PACK)
        base01 = keep.tile([P, 2, R], F32, name="base01")
        detail01 = keep.tile([P, 2, R], F32, name="detail01")
        for j in range(2):
            fetch(detail01[:, j, :], ub_t[j], l4[:], hb_t, j)
            fetch(base01[:, j, :], ua_t[j], l3[:], ha_t, j)
        nc.vector.tensor_tensor(
            wc_v[:, :, 0:2, :],
            base01[:].rearrange("p j (m t) -> p m j t", t=PACK),
            detail01[:].rearrange("p j (m t) -> p m j t", t=PACK),
            ALU.add,
        )
        base2 = keep.tile([P, R], F32, name="base2")
        detail2 = keep.tile([P, R], F32, name="detail2")
        fetch(detail2[:], ub_t[2], l4[:], hb_t, 2)
        fetch(base2[:], ua_t[2], l3[:], ha_t, 2)
        nc.vector.tensor_tensor(
            wc_v[:, :, 2, :],
            base2[:].rearrange("p (m t) -> p m t", t=PACK),
            detail2[:].rearrange("p (m t) -> p m t", t=PACK),
            ALU.add,
        )
        base3 = keep.tile([P, R], F32, name="base3")
        detail3 = keep.tile([P, R], F32, name="detail3")
        fetch(detail3[:], ub_t[3], l4[:], hb_t, 3)

        def fetch_base3(r0, r1):
            fetch(base3[:, r0:r1], ua_t[3], l3[:, r0 // PER_COLUMN : r1 // PER_COLUMN], ha_t, 3)

        def add_last(t, r0, r1):
            nc.vector.tensor_tensor(
                wc_v[:, r0 // PACK : r1 // PACK, 3, t],
                base3[:, r0 + t : r1 : PACK],
                detail3[:, r0 + t : r1 : PACK],
                ALU.add,
            )

        a_t = []

        def first_product(t):
            wc_w = keep.tile([P, P], U32, name="wc_w%d" % t, align_bytes=64)
            wc_s = keep.tile([P, P], U8, name="wc_s%d" % t, align_bytes=64)
            nc.vector.quantize_mx(
                out=wc_w[:].bitcast(FP8X4), scales=wc_s[:], in_=wc[:, t * R : (t + 1) * R]
            )
            acc = psum.tile([P, J], F32, name="acc_a%d" % t)
            nc.tensor.matmul_mx(
                out=acc[:], lhsT=wc_w[:].bitcast(FP8X4), lhsT_scale=wc_s[:],
                rhs=xc_w[:].bitcast(FP8X4), rhs_scale=xc_s[:], start=True, stop=True,
            )
            a_t.append((acc, keep.tile([P, J], F32, name="a%d" % t)))

        fetch_base3(0, CUT_A)
        add_last(0, 0, CUT_A)
        add_last(1, 0, CUT_T1)
        fetch_base3(CUT_A, CUT_B)
        add_last(0, CUT_A, CUT_B)
        fetch_base3(CUT_B, R)
        add_last(0, CUT_B, R)
        add_last(1, CUT_T1, R)
        first_product(0)
        first_product(1)
        add_last(2, 0, R)
        add_last(3, 0, R)
        first_product(2)
        first_product(3)
        for t, (acc, a) in enumerate(a_t):
            if t == 0:
                nc.scalar.copy(a[:], acc[:])
            else:
                nc.vector.tensor_copy(a[:], acc[:])

        xg_w = keep.tile([P, O], U32, name="xg_w", align_bytes=64, tag="wc")
        xg_s = keep.tile([P, O], U8, name="xg_s", align_bytes=64)
        nc.vector.tensor_copy(xg_w[:], xr_w[:].bitcast(U32).indirect(l7[:]))
        nc.vector.tensor_copy(xg_s[:], xr_s[:].indirect(l7[:]))
        acc_o = [psum.tile([P, O], F32, name="acc_o%d" % h) for h in range(2)]
        for h in range(2):
            nc.tensor.matmul_mx(
                out=acc_o[h][:], lhsT=ws_w[:, h * P : (h + 1) * P].bitcast(FP8X4),
                lhsT_scale=ws_s[:, h * P : (h + 1) * P],
                rhs=xg_w[:].bitcast(FP8X4), rhs_scale=xg_s[:], start=True, stop=False,
            )

        h_first = keep.tile([P, PACK, O], F32, name="h_first")
        h_second = keep.tile([P, PACK, O], F32, name="h_second")
        for t in range(PACK - 1):
            fetch(h_first[:, t, :], a_t[t][1], l5[:], sa_t, t)
            fetch(h_second[:, t, :], a_t[t][1], l6[:], sb_t, t)
        hid_w = keep.tile([P, O], U32, name="hid_w", align_bytes=64)
        hid_s = keep.tile([P, O], U8, name="hid_s", align_bytes=64)
        half, last = O // 2, PACK - 1
        halves = [slice(h * half, (h + 1) * half) for h in range(2)]
        hid = [
            keep.tile([P, half * PACK], BF16, name="hid%d" % h, align_bytes=64, tag=("xr_w", "xr_s")[h])
            for h in range(2)
        ]
        for h, cols in enumerate(halves):
            nc.vector.tensor_tensor(
                hid[h][:].rearrange("p (c i t) -> p c t i", i=LINE, t=PACK)[:, :, 0:last, :],
                h_first[:, 0:last, cols].rearrange("p t (c i) -> p c t i", i=LINE),
                h_second[:, 0:last, cols].rearrange("p t (c i) -> p c t i", i=LINE),
                ALU.max,
            )
        fetch(h_first[:, last, :], a_t[last][1], l5[:], sa_t, last)
        for h, cols in enumerate(halves):
            entries = slice(h * half // PER_COLUMN, (h + 1) * half // PER_COLUMN)
            fetch(h_second[:, last, cols], a_t[last][1], l6[:, entries], sb_t, last)
            nc.vector.tensor_tensor(
                hid[h][:, last::PACK], h_first[:, last, cols], h_second[:, last, cols], ALU.max
            )
        for h, cols in enumerate(halves):
            nc.vector.quantize_mx(out=hid_w[:, cols].bitcast(FP8X4), scales=hid_s[:, cols], in_=hid[h][:])

        for h in range(2):
            nc.tensor.matmul_mx(
                out=acc_o[h][:], lhsT=wb_w[:, 2 * h * P : 2 * (h + 1) * P].bitcast(FP4X4),
                lhsT_scale=wb_s[:, h * P : (h + 1) * P],
                rhs=hid_w[:].bitcast(FP8X4), rhs_scale=hid_s[:], start=False, stop=True,
            )
            result = keep.tile([P, O], F32, name="result%d" % h)
            if h == 0:
                nc.vector.tensor_copy(result[:], acc_o[h][:])
                nc.sync.dma_start(out[h * P : (h + 1) * P, :], result[:])
            else:
                nc.scalar.copy(result[:], acc_o[h][:])
                nc.scalar.dma_start(out[h * P : (h + 1) * P, :], result[:])
